import numpy as np
import ml_dtypes


def mxq(x, axis, fmt="e4m3"):
    dtype, down = {"e4m3": (ml_dtypes.float8_e4m3fn, 7), "e5m2": (ml_dtypes.float8_e5m2, 14)}[fmt]
    v = np.moveaxis(np.asarray(x, np.float32).astype(ml_dtypes.bfloat16).astype(np.float64), axis, -1)
    blocks = v.reshape(v.shape[:-1] + (-1, 32))
    amax = np.abs(blocks).max(-1, keepdims=True)
    byte = np.maximum(np.where(amax > 0, np.frexp(amax)[1] - 1 + 127, 0) - down, 1)
    scale = np.exp2(byte - 127.0)
    codes = (blocks / scale).astype(np.float32).astype(dtype).astype(np.float64)
    return np.moveaxis((codes * scale).reshape(v.shape), -1, axis)


WIDE = False


def mx_kscale(k):
    if not WIDE:
        return np.ones(k)
    levels = np.array([10, -10, 5, -5, 0])
    if k % 512:
        return np.exp2(np.random.permutation(np.resize(levels, k // 32))).repeat(32)
    a = np.empty((k // 512, 16))
    for p in range(k // 512):
        a[p, :8] = np.random.permutation(np.resize(levels, 8))
        for g in range(8):
            far = levels[np.abs(levels - a[p, g]) >= 10]
            a[p, g + 8] = far[np.random.randint(len(far))]
    return np.exp2(a.ravel()).repeat(32)


BF16 = ml_dtypes.bfloat16


def bf(x):
    return np.asarray(x, np.float32).astype(BF16)


def f64(x):
    return np.asarray(x).astype(np.float64)


H, W, D, F = 8, 1024, 512, 128
P = 2
L = W + W // P
DISP_STEP = 128.0
WIDTH0 = 128.0
WIDTH1 = 256.0


def scanline_correlation(f_left, f_right):
    d = f_left.shape[-1]
    prod = mxq(f_left, 2, "e4m3") @ mxq(f_right, 2, "e4m3").transpose(0, 2, 1)
    return prod / np.sqrt(d)


def pool_pairs(corr):
    h, w, n = corr.shape
    return np.mean(corr.reshape(h, w, n // P, P), axis=-1)


def gaussian_window(pos, ctr, width):
    t = (pos[None, None, :] - ctr[:, :, None]) / width
    return np.exp(-0.5 * t ** 2)


def draw0():
    s, t = mx_kscale(D), mx_kscale(L)
    return {
        "f_left": bf(np.random.standard_normal((H, W, D)) * s),
        "f_right": bf(np.random.standard_normal((H, W, D)) / s),
        "disp": bf(np.random.uniform(0.0, 2.0, (H, W))),
        "gain": bf((1.0 + 0.1 * np.random.standard_normal(L)) * t),
        "w_corr": bf(np.random.standard_normal((L, F)) * 3.135 / np.sqrt(L) / t[:, None]),
        "w_disp": bf(np.random.standard_normal(F)),
        "b_mot": bf(np.random.standard_normal(F) * 0.3),
    }


def core(f_left, f_right, disp, gain, w_corr, w_disp, b_mot):
    f_left, f_right, disp, gain = f64(f_left), f64(f_right), f64(disp), f64(gain)
    w_corr, w_disp, b_mot = f64(w_corr), f64(w_disp), f64(b_mot)
    w = f_left.shape[1]

    corr = scanline_correlation(f_left, f_right)

    half = pool_pairs(corr)

    i = np.arange(w, dtype=np.float64)
    ctr = i[None, :] - DISP_STEP * disp

    j0 = np.arange(w, dtype=np.float64)
    j1 = np.arange(w // P, dtype=np.float64)
    win0 = gaussian_window(j0, ctr, WIDTH0)
    win1 = gaussian_window(2.0 * j1 + 0.5, ctr, WIDTH1)

    c = np.concatenate([win0 * corr, win1 * half], axis=-1)

    cg = c * gain

    pre = (mxq(cg, 2, "e4m3") @ mxq(w_corr, 0, "e4m3")) + (disp - 1.0)[..., None] * w_disp + b_mot
    return np.maximum(pre, 0.0)


def e4m3fn_bytes(y):
    return np.clip(np.asarray(y, np.float64), -448.0, 448.0).astype(np.float32).astype(ml_dtypes.float8_e4m3fn).view(np.uint8)


def e4m3fn_values(b):
    return np.asarray(b, np.uint8).view(ml_dtypes.float8_e4m3fn).astype(np.float64)


def setup_inputs():
    d = draw0()
    x0 = np.asarray(d['f_right']).astype(np.float64)
    s = (np.max(np.abs(x0), axis=(0, 1), keepdims=True) / 448.0).astype(np.float32)
    out = {}
    for k, v in d.items():
        if k == 'f_right':
            out['f_right_bytes'] = e4m3fn_bytes(x0 / s.astype(np.float64))
            out['f_right_scale'] = s
        else:
            out[k] = v
    return out


def reference(f_left, f_right_bytes, f_right_scale, disp, gain, w_corr, w_disp, b_mot):
    return core(f_left, e4m3fn_values(f_right_bytes) * f_right_scale.astype(np.float64), disp, gain, w_corr, w_disp, b_mot)

import math
from contextlib import ExitStack

import concourse.mybir as mybir
from concourse.masks import make_identity

H, W, D, F = 8, 1024, 512, 128
L = W + W // 2
FLOPS = 2 * H * W * W * D + 2 * H * W * L * F

F32 = mybir.dt.float32
BF16 = mybir.dt.bfloat16
I32 = mybir.dt.int32
U32 = mybir.dt.uint32
U8 = mybir.dt.uint8
FP8 = mybir.dt.float8_e4m3fn
FP8X4 = mybir.dt.float8_e4m3fn_x4
ALU = mybir.AluOpType
AF = mybir.ActivationFunctionType

P = 128
NB = 8
STEPS = 24
LEAD = 2
CFG = {'qc': 0, 'sb': 1, 'ep': 3, 'rs': -9, 'rsd': 5, 'tl': (-2, 2), 'el': (-1, -1, 6, 4), 'tr': (7, 12), 'er': (8, 8, 13, 16), 'ql': (14, 19), 'qr': (17, 20), 'w': (1, -1, 0), 'wd': (0.625, 0.875, 0.75), 'va': 1, 'pm': 2, 'lr': -31, 'll': -20}
HEAD = {'rs': -3, 'rsd': 0, 'w': 1, 'tl': (-5, -2), 'el': (-3, -2, -2, 0), 'tr': (1, 6), 'er': (4, 6, 8, 9), 'ql': (11, 11), 'qr': (15, 15), 'gl': 4, 'gc': 8, 'x': (11, 22), 'pk': -7, 'lc': 3, 'ao': 8, 'sx': 25, 'ls': -6}
PIECES = (0, 64, 96)
FMAX = 3.4028234663852886e38


def source(y, g, t):
    if y == 0:
        return "V" if g == 0 or t == 3 else "S"
    if (y, g) == (1, 0):
        return "V" if t == 3 else "S"
    if t < (2 if g < 2 or y in (3, 5) else 1):
        return "P"
    return "S"


def tile_stereocorrpyramidmotionencoder_t_kernel(
    tc, f_left, f_right_bytes, f_right_scale, disp, gain, w_corr, w_disp, b_mot, out
):
    nc = tc.nc
    with ExitStack() as ctx:
        const = ctx.enter_context(tc.tile_pool(name="const", bufs=1))
        pool = ctx.enter_context(tc.tile_pool(name="work", bufs=1))
        psum = ctx.enter_context(tc.psum_pool(name="psum", bufs=1))
        ctx.enter_context(tc.manual_schedule())

        st = {}

        def load_r(y):
            rb = pool.tile([P, NB * D], U8, tag="rb", bufs=2, name="rb", align_bytes=64)
            src = f_right_bytes[y].rearrange("(p r) d -> p (r d)", p=P)
            if y == 0:
                for c in (0, 1):
                    cs = slice(c * 2048, (c + 1) * 2048)
                    nc.sync.dma_start(out=rb[:, cs], in_=src[:, cs])
            else:
                nc.sync.dma_start(out=rb[:], in_=src)
            st["rb", y] = rb

        def load_l(y):
            lr = pool.tile([P, NB * D], BF16, tag="lr", bufs=2, name="lr", align_bytes=64)
            src = f_left[y].rearrange("(p r) d -> p (r d)", p=P)
            for c in (0, 1):
                cs = slice(c * 2048, (c + 1) * 2048)
                nc.sync.dma_start(out=lr[:, cs], in_=src[:, cs])
            st["lr", y] = lr

        disp_rows = const.tile([H, W], BF16, name="disp_rows")
        nc.sync.dma_start(out=disp_rows[:], in_=disp)
        scale_row = const.tile([P, 2, D], F32, name="scale_row")
        nc.sync.dma_start(
            out=scale_row[:, 0, :],
            in_=f_right_scale.rearrange("a o k -> (a o k)").partition_broadcast(P),
        )
        load_r(0)
        disp0 = const.tile([P, W], BF16, name="disp0")
        nc.sync.dma_start(out=disp0[:], in_=disp[0].partition_broadcast(P))
        load_l(0)

        gain_f = const.tile([P, 8], BF16, name="gain_f")
        gain_h = const.tile([P, 4], BF16, name="gain_h")
        gsrc_f = gain[0:W].rearrange("(b g q t) -> q b g t", g=2, q=8, t=4)
        gsrc_h = gain[W:L].rearrange("(b g q s) -> q b g s", g=2, q=8, s=2)
        for q in range(8):
            nc.scalar.dma_start(
                out=gain_f[q:P:8, :].rearrange("b (g t) -> b g t", g=2), in_=gsrc_f[q]
            )
            nc.scalar.dma_start(
                out=gain_h[q:P:8, :].rearrange("b (g s) -> b g s", g=2), in_=gsrc_h[q]
            )
        disp_out = const.tile([P, H, NB], BF16, name="disp_out")
        wd_b = const.tile([P, F], BF16, name="wd_b")
        bm_b = const.tile([P, F], BF16, name="bm_b")
        w_raw_f = const.tile([P, 2, 4 * F], BF16, name="w_raw_f")
        w_raw_h = const.tile([P, 2, 2 * F], BF16, name="w_raw_h")

        def load_small():
            nc.sync.dma_start(out=disp_out[:], in_=disp.rearrange("y (p r) -> p y r", p=P))
            nc.sync.dma_start(out=wd_b[:], in_=w_disp.partition_broadcast(P))
            nc.sync.dma_start(out=bm_b[:], in_=b_mot.partition_broadcast(P))
            wsrc_f = w_corr[0:W].rearrange("(b g q t) f -> q b g (t f)", g=2, q=8, t=4)
            wsrc_h = w_corr[W:L].rearrange("(b g q s) f -> q b g (s f)", g=2, q=8, s=2)
            for q in range(8):
                nc.sync.dma_start(out=w_raw_f[q:P:8, :, :], in_=wsrc_f[q])
                nc.sync.dma_start(out=w_raw_h[q:P:8, :, :], in_=wsrc_h[q])

        ident = const.tile([P, P], F32, name="ident")
        make_identity(nc, ident[:])
        part_i = const.tile([P, 1], I32, name="part_i")
        nc.gpsimd.iota(part_i[:], pattern=[[0, 1]], base=0, channel_multiplier=1)

        def ramp(name, width, pattern, base, step, view=None):
            r = const.tile([P, width], F32, name=name)
            nc.gpsimd.iota(
                view(r) if view else r[:], pattern=pattern, base=base, channel_multiplier=step,
                allow_small_or_imprecise_dtypes=True,
            )
            return r

        def affine(dst, src, mul, add):
            nc.gpsimd.tensor_scalar(dst, src, mul, add, op0=ALU.mult, op1=ALU.add)

        pos_t = ramp("pos", W, [[1, NB], [NB, P]], 0, 0)
        for c in (0, 1):
            affine(pos_t[:, 512 * c : 512 * (c + 1)], pos_t[:, 512 * c : 512 * (c + 1)], 1.0 / 128.0, 0.0)
        pos = pos_t[:].rearrange("p (r q) -> p r q", r=NB)

        park_all = out[H - 1, W - 3 * H * W // F : W, :].rearrange("(k y a) f -> k y (a f)", k=3, y=H)
        park = park_all[0]
        four = const.tile([P, 1], F32, name="four")
        nc.gpsimd.memset(four[:], 4.0)
        x_arg = pool.tile([P, W], F32, tag="ftmp", bufs=1, name="x_arg")

        def park_rows():
            e_rows = const.tile([H, NB, P], F32, name="e_rows")
            nc.vector.tensor_tensor(
                out=e_rows[:],
                in0=disp_rows[:].rearrange("y (p r) -> y r p", r=NB),
                in1=pos[0:H],
                op=ALU.subtract,
            )
            er = e_rows[:].rearrange("y r p -> y (r p)")
            nc.sync.dma_start(out=park_all[0], in_=er)
            rows = const.tile([H, 2, W], F32, name="rows")
            nc.scalar.activation(out=rows[:, 0], in_=er, func=AF.Identity, bias=four[0:H, 0:1])
            nc.scalar.activation(out=rows[:, 1], in_=er, func=AF.Square, bias=four[0:H, 0:1])
            nc.sync.dma_start(out=park_all[1], in_=rows[:, 0])
            nc.sync.dma_start(out=park_all[2], in_=rows[:, 1])

        nc.gpsimd.memset(x_arg[:], 0.0)

        def load_x():
            for base in PIECES:
                for n, kind in enumerate((1, 1, 2)):
                    nc.sync.dma_start(out=x_arg[base + 8 * n : base + 8 * n + H, :], in_=park_all[kind])

        e0 = pool.tile([P, W], F32, tag="e", bufs=2, name="e0", align_bytes=64)
        st["e", 0] = e0

        def first_e(c):
            nc.gpsimd.tensor_tensor(
                out=e0[:].rearrange("p (r q) -> p r q", r=NB)[:, 4 * c : 4 * c + 4, :],
                in0=disp0[:].rearrange("p (q r) -> p r q", r=NB)[:, 4 * c : 4 * c + 4, :],
                in1=pos[:, 4 * c : 4 * c + 4, :],
                op=ALU.subtract,
            )

        first_e(0)
        first_e(1)

        lnr = const.tile([P, 12], F32, name="lnr")

        def gain_log():
            gabs = const.tile([P, 12], F32, name="gabs")
            for ks, src in ((slice(0, 8), gain_f), (slice(8, 12), gain_h)):
                nc.vector.scalar_tensor_tensor(
                    out=gabs[:, ks], in0=src[:], scalar=-1.0, in1=src[:], op0=ALU.mult, op1=ALU.max
                )
            gsafe = const.tile([P, 12], F32, name="gsafe")
            nc.vector.tensor_scalar(gsafe[:], gabs[:], 2.0**-60, None, op0=ALU.max)
            nc.scalar.activation(out=lnr[:], in_=gsafe[:], func=AF.Ln)

        sub_i = const.tile([P, 1], I32, name="sub_i")
        nc.vector.tensor_single_scalar(sub_i[:], part_i[:], 3, op=ALU.arith_shift_right)
        sub_f = const.tile([P, 1], F32, name="sub_f")
        nc.vector.tensor_scalar(sub_f[:], sub_i[:], 0.25, None, op0=ALU.mult)
        jf = ramp("jf", 8, [[32, 2], [1, 4]], 0, 4)
        jh = ramp("jh", 4, [[64, 2], [4, 2]], 1, 8)
        jm = const.tile([P, 12], F32, name="jm")
        affine(jm[:, 0:8], jf[:], 1.0 / 128.0, sub_f[:, 0:1])
        affine(jm[:, 8:12], jh[:], 1.0 / 256.0, sub_f[:, 0:1])
        lng = const.tile([P, 12], F32, name="lng")
        lng2 = const.tile([P, 12], F32, name="lng2")
        lng3 = const.tile([P, 12], F32, name="lng3")
        jm2 = const.tile([P, 12], F32, name="jm2")
        affine(jm2[:], jm[:], 2.0, 0.0)
        jc = const.tile([P, 12], F32, name="jc")
        affine(jc[:], jm[:], 1.0, -4.0)
        jsq = const.tile([P, 12], F32, name="jsq")
        nc.gpsimd.tensor_tensor(out=jsq[:], in0=jm[:], in1=jm[:], op=ALU.mult)
        jcsq = const.tile([P, 12], F32, name="jcsq")
        nc.gpsimd.tensor_tensor(out=jcsq[:], in0=jc[:], in1=jc[:], op=ALU.mult)

        def gain_consts():
            c_f = -0.5 * math.log(512.0)
            c_h = -0.5 * math.log(512.0) - math.log(2.0)
            for ks, cst, f in ((slice(0, 8), c_f, -0.5), (slice(8, 12), c_h, -0.125)):
                nc.vector.tensor_scalar(lng[:, ks], lnr[:, ks], cst, None, op0=ALU.add)
                for dst, sq in ((lng2, jsq), (lng3, jcsq)):
                    nc.vector.scalar_tensor_tensor(
                        out=dst[:, ks], in0=sq[:, ks], scalar=f, in1=lng[:, ks], op0=ALU.mult, op1=ALU.add
                    )

        def late_constants():
            nc.gpsimd.tensor_copy(out=scale_row[:, 1, :], in_=scale_row[:, 0, :])
            wd = const.tile([P, F], F32, name="wd")
            nc.gpsimd.tensor_copy(out=wd[:], in_=wd_b[:])
            bm = const.tile([P, F], F32, name="bm")
            nc.gpsimd.tensor_copy(out=bm[:], in_=bm_b[:])
            dm1 = const.tile([P, H * NB], F32, name="dm1")
            nc.gpsimd.tensor_scalar(dm1[:], disp_out[:].rearrange("p y r -> p (y r)"), 1.0, -1.0, op0=ALU.mult, op1=ALU.add)
            st["wd"], st["bm"], st["dm1"] = wd, bm, dm1

        def arg_operands():
            jhi = const.tile([P, 2, P], F32, name="jhi")
            for g in range(2):
                nc.gpsimd.iota(
                    jhi[:, g].rearrange("p (b q) -> p b q", q=8), pattern=[[64, 16], [4, 8]], base=32 * g - 512,
                    channel_multiplier=0, allow_small_or_imprecise_dtypes=True,
                )
                affine(jhi[:, g], jhi[:, g], 1.0 / 128.0, 0.0)
            rowf = ramp("rowf", H, [[-1, H]], 0, 1)

            def rows_at(offset, value, name):
                acc = const.tile([P, H], F32, name=name)
                tmp = const.tile([P, H], F32, name=name + "_tmp")
                for n, base in enumerate(PIECES):
                    nc.gpsimd.tensor_scalar(
                        (tmp if n else acc)[:], rowf[:], float(base + offset), value, op0=ALU.is_equal, op1=ALU.mult
                    )
                    if n:
                        nc.gpsimd.tensor_tensor(out=acc[:], in0=acc[:], in1=tmp[:], op=ALU.add)
                return acc

            st["jhi"] = jhi
            st["ma"], st["mb"], st["mc"] = rows_at(0, -1.0, "ma"), rows_at(8, -1.0, "mb"), rows_at(16, -0.5, "mc")
            maq = const.tile([P, H], F32, name="maq")
            affine(maq[:], st["ma"][:], 0.25, 0.0)
            st["maq"] = maq

        def split_x():
            mv = const.tile([P, W], BF16, name="mv")
            st["mv"] = mv
            for n, base in enumerate((0, 64, 96)):
                for c in range(4):
                    cs = slice(256 * c, 256 * (c + 1))
                    if n:
                        nc.gpsimd.tensor_tensor(out=x_arg[base:P, cs], in0=x_arg[base:P, cs], in1=mv[base:P, cs], op=ALU.subtract)
                    affine(mv[base:P, cs], x_arg[base:P, cs], 1.0, 0.0)

        def stationaries(y):
            for g in range(3):
                for t in range(4):
                    if source(y, g, t) != "P":
                        continue
                    f = 1.0 if g < 2 else 0.25
                    lo = (t if g < 2 else 2 * (t % 2) + 0.5) / 128.0
                    col = pool.tile([P, 1], F32, tag="sc", bufs=4, name="sc")
                    nc.gpsimd.tensor_scalar(col[:], st["mb"][:, y : y + 1], lo, st["mc"][:, y : y + 1], op0=ALU.mult, op1=ALU.add)
                    if g == 2:
                        nc.gpsimd.tensor_scalar(col[:], col[:], f, 0.0, op0=ALU.mult, op1=ALU.add)
                    am = st["ma"] if g < 2 else st["maq"]
                    sta = pool.tile([P, P], BF16, tag="sta", bufs=10, name="sta", align_bytes=64)
                    jg = g if g < 2 else t // 2
                    nc.gpsimd.tensor_scalar(sta[:], st["jhi"][:, jg], am[:, y : y + 1], col[:, 0:1], op0=ALU.mult, op1=ALU.add)
                    st["sta", y, g, t] = sta

        def weights():
            sgn = const.tile([P, 12], F32, name="sgn")
            neg = const.tile([P, 12], F32, name="neg")
            for dst, op in ((sgn, ALU.is_gt), (neg, ALU.is_lt)):
                nc.gpsimd.tensor_scalar(dst[:, 0:8], gain_f[:], 0.0, 1.0, op0=op, op1=ALU.mult)
                nc.gpsimd.tensor_scalar(dst[:, 8:12], gain_h[:], 0.0, 1.0, op0=op, op1=ALU.mult)
            nc.gpsimd.tensor_tensor(out=sgn[:], in0=sgn[:], in1=neg[:], op=ALU.subtract)
            wg = const.tile([P, 3, F, 4], BF16, name="wg", align_bytes=64)
            for g in range(3):
                if g < 2:
                    src = w_raw_f[:, g, :].rearrange("p (t f) -> p f t", t=4)
                else:
                    src = w_raw_h[:].rearrange("p g (s f) -> p f (g s)", s=2)
                nc.gpsimd.tensor_tensor(
                    out=wg[:, g],
                    in0=src,
                    in1=sgn[:, 4 * g : 4 * g + 4].unsqueeze(1).to_broadcast([P, F, 4]),
                    op=ALU.mult,
                )
            st["wg"] = wg

        def weights_q():
            wg = st["wg"]
            wc = const.tile([P, 3, F], U32, name="wc", align_bytes=64)
            ws = const.tile([P, 3, F], U8, name="ws", align_bytes=64)
            for g in range(3):
                nc.vector.quantize_mx(
                    out=wc[:, g].bitcast(FP8X4), scales=ws[:, g], in_=wg[:, g].rearrange("p f t -> p (f t)")
                )
            st["wc"], st["ws"] = wc, ws

        def rscale(y, c):
            rb = st["rb", y]
            if c == 0:
                rs0 = pool.tile([P, NB * D], BF16, tag="rs", bufs=2, name="rs", align_bytes=64)
                st["rs", y] = rs0
            rs = st["rs", y]
            width = D if y == 0 else 2 * D
            sc = scale_row[:].rearrange("p a d -> p (a d)")[:, 0:width]
            for k in range(2 * D // width):
                cs = slice(2 * D * c + k * width, 2 * D * c + (k + 1) * width)
                nc.vector.tensor_tensor(out=rs[:, cs], in0=rb[:, cs].bitcast(FP8), in1=sc, op=ALU.mult)

        def tr(src, blocks, key):
            bank = psum.tile([P, 4 * P], F32, tag="tr", bufs=2, name="trb")
            words = src[:].bitcast(F32)
            for x, r in enumerate(blocks):
                for u in (0, 1):
                    o = (2 * x + u) * P
                    nc.tensor.transpose(bank[:, o : o + P], words[:, 256 * r + u : 256 * (r + 1) : 2], ident[:])
            st[key] = bank

        def tr_r(y, t):
            tr(st["rs", y], (t, t + 4), ("tr_r", y, t))

        def tr_l(y, a):
            tr(st["lr", y], (2 * a, 2 * a + 1), ("tr_l", y, a))

        def ev_r(y, t):
            if t == 0:
                rg0 = pool.tile([P, W * 4], BF16, tag="rg", bufs=1, name="rg", align_bytes=64)
                st["rg", y] = rg0
            rg = st["rg", y][:].bitcast(F32)
            src = st.pop(("tr_r", y, t))[:].rearrange("p (x b g h) -> p g b h x", x=4, g=2, h=4)
            for g in (0, 1):
                o = (4 * g + t) * 256
                nc.scalar.copy(
                    out=rg[:, o : o + 256].rearrange("p (b h x) -> p b h x", b=16, h=4),
                    in_=src[:, g],
                )

        def ev_l(y, a):
            if a == 0:
                lg0 = pool.tile([P, W * 4], BF16, tag="lg", bufs=1, name="lg", align_bytes=64)
                st["lg", y] = lg0
            lg = st["lg", y][:].bitcast(F32)
            src = st.pop(("tr_l", y, a))[:].rearrange("p (x u q) -> p x q u", x=2, u=2)
            nc.scalar.copy(
                out=lg[:, 512 * a : 512 * (a + 1)].rearrange("p (x q u) -> p x q u", x=2, u=2), in_=src
            )

        def q_rl(y, side, h):
            if h == 0:
                c0 = pool.tile([P, W], U32, tag=side + "c", bufs=2, name="oc", align_bytes=64)
                s0 = pool.tile([P, W], U8, tag=side + "x", bufs=2, name="ox", align_bytes=64)
                st[side + "c", y], st[side + "x", y] = c0, s0
            cs = slice(512 * h, 512 * (h + 1))
            nc.vector.quantize_mx(
                out=st[side + "c", y][:, cs].bitcast(FP8X4),
                scales=st[side + "x", y][:, cs],
                in_=st[side + "g", y][:, 2048 * h : 2048 * (h + 1)],
            )

        def load_e(y):
            e = pool.tile([P, W], F32, tag="e", bufs=2, name="e", align_bytes=64)
            nc.sync.dma_start(out=e[:], in_=park[y].partition_broadcast(P))
            st["e", y] = e

        def win_tile(y, g):
            wt = pool.tile([P, 4, W], F32, tag="w", bufs=3, name="wt", align_bytes=64)
            st["w", y, g] = wt

        def win_arg(y, g, t, a, b):
            k = 4 * g + t
            e, wt = st["e", y], st["w", y, g]
            if source(y, g, t) == "V":
                nc.vector.scalar_tensor_tensor(
                    out=wt[:, t, a:b], in0=e[:, a:b], scalar=jm2[:, k : k + 1], in1=e[:, a:b], op0=ALU.add, op1=ALU.mult
                )
            else:
                nc.scalar.activation(out=wt[:, t, a:b], in_=e[:, a:b], func=AF.Square, bias=jm[:, k : k + 1])

        def win_mm(y, g, t, h):
            bank = psum.tile([P, 512], F32, tag="arg", bufs=2, name="argb")
            nc.tensor.matmul(
                bank[:], lhsT=st["sta", y, g, t][:], rhs=st["mv"][:, 512 * h : 512 * (h + 1)], start=True, stop=True
            )
            st["arg", y, g, t, h] = bank

        def win_exp(y, g, t, a, b):
            k = 4 * g + t
            wt = st["w", y, g]
            ln = lng2 if source(y, g, t) == "V" else lng
            nc.scalar.activation(
                out=wt[:, t, a:b], in_=wt[:, t, a:b], func=AF.Exp, bias=ln[:, k : k + 1], scale=-0.5 if g < 2 else -0.125
            )

        def win_exp_p(y, g, t, h):
            k = 4 * g + t
            nc.scalar.activation(
                out=st["w", y, g][:, t, 512 * h : 512 * (h + 1)],
                in_=st.pop(("arg", y, g, t, h))[:],
                func=AF.Exp,
                bias=lng3[:, k : k + 1],
            )

        def corr(y, n):
            g, ib = divmod(n, NB)
            bank = psum.tile([P, 4, P], F32, tag="corr", bufs=3, name="corr")
            lc, ls = st["lc", y], st["lx", y]
            rc, rsc = st["rc", y], st["rx", y]
            ics = slice(ib * P, (ib + 1) * P)
            for t in range(4):
                tiles = (4 * g + t,) if g < 2 else (2 * t, 2 * t + 1)
                for x, m in enumerate(tiles):
                    ms = slice(m * P, (m + 1) * P)
                    nc.tensor.matmul_mx(
                        out=bank[:, t, :],
                        lhsT=rc[:, ms].bitcast(FP8X4),
                        lhsT_scale=rsc[:, ms],
                        rhs=lc[:, ics].bitcast(FP8X4),
                        rhs_scale=ls[:, ics],
                        start=(x == 0),
                        stop=(x == len(tiles) - 1),
                    )
            st["corr", y, n] = bank

        def mult(y, n):
            g, ib = divmod(n, NB)
            h, x = divmod(ib, 4)
            if x == 0:
                cg0 = pool.tile([P, 4 * P, 4], BF16, tag="cg", bufs=4, name="cg", align_bytes=64)
                st["cg", y, g, h] = cg0
            cg = st["cg", y, g, h]
            bank = st.pop(("corr", y, n))
            wt = st["w", y, g][:, :, ib * P : (ib + 1) * P]
            nc.vector.tensor_tensor(
                out=cg[:, x * P : (x + 1) * P, :].rearrange("p (c i) t -> p c t i", i=2),
                in0=bank[:].rearrange("p t (c i) -> p c t i", i=2),
                in1=wt.rearrange("p t (c i) -> p c t i", i=2),
                op=ALU.mult,
            )

        def q_c(y, g, h):
            cc = pool.tile([P, 4 * P], U32, tag="cc", bufs=8, name="cc", align_bytes=64)
            cs = pool.tile([P, 4 * P], U8, tag="cs", bufs=8, name="cs", align_bytes=64)
            cg = st.pop(("cg", y, g, h))
            nc.vector.quantize_mx(out=cc[:].bitcast(FP8X4), scales=cs[:], in_=cg[:].rearrange("p i t -> p (i t)"))
            st["cc", y, g, h] = (cc, cs)

        def stage_b(y, h):
            bank = psum.tile([P, 4, F], F32, tag="ob", bufs=1, name="ob")
            wc, ws = st["wc"], st["ws"]
            for x in range(4):
                xs = slice(x * P, (x + 1) * P)
                for g in range(3):
                    cc, cs = st["cc", y, g, h]
                    nc.tensor.matmul_mx(
                        out=bank[:, x, :],
                        lhsT=cc[:, xs].bitcast(FP8X4),
                        lhsT_scale=cs[:, xs],
                        rhs=wc[:, g].bitcast(FP8X4),
                        rhs_scale=ws[:, g],
                        start=(g == 0),
                        stop=(g == 2),
                    )
            st["ob", y, h] = bank

        def bias(y, h):
            t1 = pool.tile([P, 4, F], F32, tag="t1", bufs=2, name="t1")
            wd, bm, dm1 = st["wd"], st["bm"], st["dm1"]
            for x in range(4):
                k = y * NB + 4 * h + x
                nc.gpsimd.tensor_scalar(t1[:, x, :], wd[:], dm1[:, k : k + 1], 0.0, op0=ALU.mult, op1=ALU.add)
            nc.gpsimd.tensor_tensor(out=t1[:], in0=t1[:], in1=bm[:].unsqueeze(1).to_broadcast([P, 4, F]), op=ALU.add)
            st["t1", y, h] = t1

        def epi(y, h):
            u = pool.tile([P, 4 * F], F32, tag="u", bufs=2, name="u")
            nc.vector.tensor_tensor(
                out=u[:],
                in0=st.pop(("ob", y, h))[:].rearrange("p x f -> p (x f)"),
                in1=st.pop(("t1", y, h))[:].rearrange("p x f -> p (x f)"),
                op=ALU.add,
            )
            st["u", y, h] = u

        def fin(y, h):
            u = st.pop(("u", y, h))
            o = pool.tile([P, 4 * F], F32, tag="o", bufs=2, name="o")
            nc.gpsimd.tensor_scalar(o[:], u[:], 0.0, FMAX, op0=ALU.max, op1=ALU.min)
            dst = out[y].rearrange("(p r) f -> p r f", p=P)[:, 4 * h : 4 * h + 4, :]
            nc.sync.dma_start(out=dst, in_=o[:].rearrange("p (x f) -> p x f", x=4))

        plan = {}

        def at(step, fn, *args):
            plan.setdefault(step, []).append((fn, args))

        for y in range(H):
            b = STEPS * y
            for n in range(STEPS):
                at(b + n - LEAD, corr, y, n)
        for y in range(H):
            b = STEPS * y
            for n in range(STEPS):
                at(b + n, mult, y, n)
        for y in range(H):
            b = STEPS * y
            for g in range(3):
                for h in range(2):
                    at(b + 8 * g + 4 * h + 3 + CFG["qc"], q_c, y, g, h)
            for h in range(2):
                at(b + 8 + 4 * h, bias, y, h)
                at(b + 20 + 4 * h + CFG["sb"], stage_b, y, h)
                at(b + 20 + 4 * h + CFG["ep"], epi, y, h)
                at(b + 20 + 4 * h + CFG["ep"] + 1, fin, y, h)
        for y in range(H):
            b = STEPS * (y - 1)
            c = CFG if y else HEAD
            if y:
                at(b + CFG["lr"], load_r, y)
                at(b + CFG["ll"], load_l, y)
                at(b + 2, load_e, y)
                at(b + 8, stationaries, y)
            for x, ch in enumerate((0, 2, 1, 3)):
                at(b + c["rs"] + x * c["rsd"], rscale, y, ch)
            for x in range(2):
                for z in range(2):
                    at(b + c["tl"][x], tr_l, y, 2 * x + z)
                    at(b + c["el"][2 * x + z], ev_l, y, 2 * x + z)
                    at(b + c["tr"][x], tr_r, y, 2 * x + z)
                    at(b + c["er"][2 * x + z], ev_r, y, 2 * x + z)
                at(b + c["ql"][x], q_rl, y, "l", x)
                at(b + c["qr"][x], q_rl, y, "r", x)
            for g in range(3):
                s0 = b + 16 + 8 * g
                if y == 0 and g == 0:
                    at(HEAD["w"] - 25, win_tile, y, g)
                    for c2 in (0, 1):
                        for t in range(4):
                            at(HEAD["w"] - 24 + c2, win_arg, y, g, t, 512 * c2, 512 * (c2 + 1))
                            at(HEAD["x"][c2] - 24, win_exp, y, g, t, 512 * c2, 512 * (c2 + 1))
                    continue
                at(s0 - 1, win_tile, y, g)
                kinds = [source(y, g, t) for t in range(4)]
                pe = [t for t in range(4) if kinds[t] == "P"]
                other = [t for t in range(4) if kinds[t] != "P"]
                units = [("a", other[0])]
                for x, t in enumerate(other):
                    if pe:
                        units.append(("p", pe.pop(0)))
                    if x + 1 < len(other):
                        units.append(("a", other[x + 1]))
                    units.append(("e", t))
                for x, (kind, t) in enumerate(units):
                    s = s0 + CFG["w"][g] + x * CFG["wd"][g]
                    if kind == "a":
                        at(int(s) - (CFG["va"] if kinds[t] == "V" else 0), win_arg, y, g, t, 0, W)
                    elif kind == "e":
                        at(int(s), win_exp, y, g, t, 0, W)
                    else:
                        for h in (0, 1):
                            at(int(s) - CFG["pm"], win_mm, y, g, t, h)
                            at(int(s), win_exp_p, y, g, t, h)
        at(HEAD["ls"] - 24, load_small)
        at(HEAD["gl"] - 24, gain_log)
        at(HEAD["gc"] - 24, gain_consts)
        at(HEAD["pk"] - 24, park_rows)
        at(HEAD["pk"] - 23, load_x)
        at(HEAD["sx"] - 24, split_x)
        at(HEAD["lc"] - 24, late_constants)
        at(HEAD["ao"] - 24, arg_operands)
        at(HEAD["ao"] - 24, weights)
        at(19, weights_q)
        for s in sorted(plan):
            for fn, args in plan[s]:
                fn(*args)
